import numpy as np
import ml_dtypes


def mxq(x, axis, fmt="e4m3"):
    dtype, down = {"e4m3": (ml_dtypes.float8_e4m3fn, 7), "e5m2": (ml_dtypes.float8_e5m2, 14)}[fmt]
    v = np.moveaxis(np.asarray(x, np.float32).astype(ml_dtypes.bfloat16).astype(np.float64), axis, -1)
    blocks = v.reshape(v.shape[:-1] + (-1, 32))
    amax = np.abs(blocks).max(-1, keepdims=True)
    byte = np.maximum(np.where(amax > 0, np.frexp(amax)[1] - 1 + 127, 0) - down, 1)
    scale = np.exp2(byte - 127.0)
    codes = (blocks / scale).astype(np.float32).astype(dtype).astype(np.float64)
    return np.moveaxis((codes * scale).reshape(v.shape), -1, axis)


WIDE = False


def mx_kscale(k):
    if not WIDE:
        return np.ones(k)
    levels = np.array([10, -10, 5, -5, 0])
    if k % 512:
        return np.exp2(np.random.permutation(np.resize(levels, k // 32))).repeat(32)
    a = np.empty((k // 512, 16))
    for p in range(k // 512):
        a[p, :8] = np.random.permutation(np.resize(levels, 8))
        for g in range(8):
            far = levels[np.abs(levels - a[p, g]) >= 10]
            a[p, g + 8] = far[np.random.randint(len(far))]
    return np.exp2(a.ravel()).repeat(32)


def f64(x):
    return np.asarray(x).astype(np.float64)


def striped(idx):
    return np.tile(idx.reshape(-1, 16).T, (8, 1)).astype(np.uint16)


def unstriped(offs):
    return offs[:16].T.reshape(-1).astype(np.int64)


E2M1 = np.array([0.0, 0.5, 1.0, 1.5, 2.0, 3.0, 4.0, 6.0, -0.0, -0.5, -1.0, -1.5, -2.0, -3.0, -4.0, -6.0])


def pack_weight(w, fmt):
    k, n = w.shape
    w = f64(np.asarray(w, np.float32).astype(ml_dtypes.bfloat16)).reshape(k // 32, 32, n)
    amax = np.abs(w).max(1)
    if fmt == "e4m3":
        byte = np.frexp(amax)[1] - 1 + 127 - 7
    else:
        mant, ex = np.frexp(amax / 6.0)
        byte = np.where(mant > 0.5, ex, ex - 1) + 127
    byte = np.clip(np.where(amax > 0, byte, 1), 1, 254)
    scaled = (w * np.exp2(127.0 - byte)[:, None, :]).reshape(k, n).astype(np.float32)
    by_word = np.ascontiguousarray(scaled.reshape(k // 512, 128, 4, n).transpose(0, 1, 3, 2))
    if fmt == "e4m3":
        words = by_word.astype(ml_dtypes.float8_e4m3fn).view(np.uint8)
    else:
        c = by_word.astype(ml_dtypes.float4_e2m1fn).view(np.uint8) & 0xF
        words = (c[..., 0::2] | (c[..., 1::2] << 4)).reshape(k // 512, 128, 2 * n)
    return np.ascontiguousarray(words), np.ascontiguousarray(byte.astype(np.uint8).reshape(k // 512, 16, n))


def unpack_weight(words, scales, fmt):
    g, _, n = scales.shape
    words = np.ascontiguousarray(words).reshape(g, 128, n, -1)
    if fmt == "e4m3":
        vals = words.view(ml_dtypes.float8_e4m3fn).astype(np.float64)
    else:
        nib = np.empty((g, 128, n, 4), np.uint8)
        nib[..., 0::2] = words & 0xF
        nib[..., 1::2] = words >> 4
        vals = E2M1[nib]
    vals = vals * np.repeat(np.exp2(scales.astype(np.float64) - 127.0), 8, axis=1)[..., None]
    return vals.transpose(0, 1, 3, 2).reshape(g * 512, n)


def gelu(v):
    return 0.5 * v * (1.0 + np.tanh(np.sqrt(2.0 / np.pi) * (v + 0.044715 * v**3)))


K, T, S, T2, P, H, M, N = 1024, 2048, 512, 2048, 1024, 512, 1024, 512

def setup_inputs():
    n = np.random.standard_normal
    s, u, u2 = mx_kscale(K)[:, None], mx_kscale(H)[:, None], mx_kscale(M)[:, None]
    perm = np.random.permutation(T2)
    d = {}
    d["tab_words"], d["tab_scales"] = pack_weight(n((K, T)) * s, "e4m3")
    d["tab2_words"], d["tab2_scales"] = pack_weight(n((K, T)) * s, "e4m3")
    d["offs"] = striped(np.random.permutation(T)[:S])
    d["offs2"] = striped(np.random.permutation(T)[:S])
    d["offs3"] = striped(perm[:S])
    d["offs4"] = striped(perm[S:2 * S])
    d["offs5"] = striped(np.random.permutation(T2)[:P])
    d["w1"] = (0.5 * n((K, H)) / K**0.5 / s).astype(np.float32)
    d["b1"] = (0.4 * n(H)).astype(np.float32)
    d["w2_words"], d["w2_scales"] = pack_weight(0.56 * n((K, H)) / K**0.5 / s, "e4m3")
    d["wg1"] = np.exp(0.3 * n((128, S))).astype(np.float32)
    d["wg2"] = np.exp(0.3 * n((128, S))).astype(np.float32)
    d["page0"] = (0.6 * n((H, T2))).astype(np.float32)
    d["gain"] = (2.0 * np.exp(0.3 * n(H)) * u[:, 0]).astype(np.float32)
    d["w3"] = (n((H, M)) / H**0.5 / u).astype(np.float32)
    d["stress"] = (np.exp(0.4 * n(M)) * u2[:, 0]).astype(np.float32)
    d["w4_words"], d["w4_scales"] = pack_weight(1.3 * n((M, N)) / M**0.5 / u2, "e2m1")
    return d

def reference(tab_words, tab_scales, tab2_words, tab2_scales, offs, offs2, offs3, offs4, offs5, w1, b1, w2_words, w2_scales, wg1, wg2, page0, gain, w3, stress, w4_words, w4_scales):
    v = unpack_weight(tab_words, tab_scales, "e4m3")[:, unstriped(offs)]
    v2 = unpack_weight(tab2_words, tab2_scales, "e4m3")[:, unstriped(offs2)]
    h1 = np.square((mxq(f64(w1), 0, "e4m3").T @ v) + f64(b1)[:, None])
    h2 = np.sin(unpack_weight(w2_words, w2_scales, "e4m3").T @ v2)
    page = f64(page0).copy()
    page[:, unstriped(offs3)] = np.tile(f64(wg1), (H // 128, 1)) * h1
    page[:, unstriped(offs4)] = np.tile(f64(wg2), (H // 128, 1)) * h2
    x = page[:, unstriped(offs5)] * f64(gain)[:, None]
    y = np.tanh(mxq(f64(w3), 0, "e4m3").T @ mxq(x, 0, "e4m3")) * f64(stress)[:, None]
    return unpack_weight(w4_words, w4_scales, "e2m1").T @ mxq(y, 0, "e4m3")

@@ -1,0 +1,330 @@
+from contextlib import ExitStack
+
+import concourse.mybir as mybir
+from concourse.masks import make_identity
+
+F32 = mybir.dt.float32
+BF16 = mybir.dt.bfloat16
+I32 = mybir.dt.int32
+U32 = mybir.dt.uint32
+U16 = mybir.dt.uint16
+U8 = mybir.dt.uint8
+FP8X4 = mybir.dt.float8_e4m3fn_x4
+FP4X4 = mybir.dt.float4_e2m1fn_x4
+ACT = mybir.ActivationFunctionType
+MULT = mybir.AluOpType.mult
+
+K, T, S, T2, NJ, H, M, N = 1024, 2048, 512, 2048, 1024, 512, 1024, 512
+FLOPS = 2 * (2 * K * H * S + H * M * NJ + M * N * NJ)
+
+P = 128
+PACK = 4
+PASSES = 2
+XC = 256
+YC = 128
+
+
+def tile_list_pipe_voicing_ledger_kernel(
+    tc, tab_words, tab_scales, tab2_words, tab2_scales, offs, offs2, offs3, offs4, offs5,
+    w1, b1, w2_words, w2_scales, wg1, wg2, page0, gain, w3, stress, w4_words, w4_scales, out,
+):
+    nc = tc.nc
+    with ExitStack() as ctx:
+        lists = ctx.enter_context(tc.tile_pool(name="lists", bufs=1))
+        keep = ctx.enter_context(tc.tile_pool(name="keep", bufs=1))
+        ring = ctx.enter_context(tc.tile_pool(name="ring", bufs=2))
+        chain = ctx.enter_context(tc.tile_pool(name="chain", bufs=1))
+        psum = ctx.enter_context(tc.psum_pool(name="psum", bufs=1))
+
+        def load_list(src, name):
+            t_ = lists.tile(list(src.shape), U16, name=name)
+            nc.sync.dma_start(t_[:], src)
+            return t_
+
+        def bank(name):
+            return psum.tile([P, PACK, P], F32, name=name, tag="bank", bufs=4)
+
+        def flat(t_):
+            return t_[:].rearrange("p a b -> p (a b)")
+
+        warm = keep.tile([P, 8], F32, name="warm")
+        nc.gpsimd.memset(warm[:, 0:1], 0.0)
+        nc.scalar.activation(out=warm[:, 1:2], in_=warm[:, 0:1], func=ACT.Silu)
+
+        def zeroed_plane(width, name):
+            t_ = keep.tile([P, width], U8, name=name, align_bytes=64)
+            nc.vector.memset(t_[:].bitcast(I32), 0)
+            return t_
+
+        w2_s = zeroed_plane(H, "w2_s")
+        tab2_s = zeroed_plane(T, "tab2_s")
+        tab_s = zeroed_plane(T, "tab_s")
+        w4_s = zeroed_plane(PASSES * N, "w4_s")
+        ident = keep.tile([P, P], F32, name="ident")
+        make_identity(nc, ident[:])
+
+        def load_packed_planes(eng, plane, scales):
+            for q in range(4):
+                eng.dma_start(plane[32 * q : 32 * q + 8, :].bitcast(I32), scales[:, 4 * q : 4 * q + 4, :].bitcast(I32))
+
+        def load_words(src, a, name, offset):
+            t_ = chain.tile([P, T], I32, name=name, offset=offset, align_bytes=64)
+            nc.sync.dma_start(t_[:], src[a].rearrange("p c i -> p (c i)").bitcast(I32))
+            return t_
+
+        def load_page(t):
+            t_ = keep.tile([P, T2], F32, name="page%d" % t)
+            nc.sync.dma_start(t_[:], page0.rearrange("(p t) s -> t p s", t=PACK)[t])
+            return t_
+
+        def load_wg(src, name):
+            t_ = keep.tile([P, S], F32, name=name)
+            nc.sync.dma_start(t_[:], src)
+            return t_
+
+        def load_w1(a):
+            t_ = keep.tile([P, PACK, H], F32, name="w1_raw%d" % a)
+            nc.sync.dma_start(t_[:], w1[512 * a : 512 * (a + 1), :].rearrange("(p j) c -> p j c", j=PACK))
+            return t_
+
+        def load_w3(a):
+            t_ = chain.tile([P, PACK + a, 512], F32, name="w3_raw%d" % a, offset=8192 * a, align_bytes=64)
+            nc.sync.dma_start(t_[:, 0:PACK, :], w3[:, 512 * a : 512 * (a + 1)].rearrange("(p j) c -> p j c", j=PACK))
+            return t_
+
+        load_packed_planes(nc.gpsimd, tab2_s, tab2_scales)
+        load_packed_planes(nc.gpsimd, tab_s, tab_scales)
+        for q in range(4):
+            nc.gpsimd.dma_start(
+                w4_s[32 * q : 32 * q + 4, :].bitcast(I32).rearrange("r (a n) -> r a n", a=PASSES),
+                w4_scales[:, 4 * q : 4 * q + 4, :].bitcast(I32).rearrange("a r n -> r a n"),
+            )
+
+        idx2 = load_list(offs2, "idx2")
+        wg2_raw = load_wg(wg2, "wg2_raw")
+        tab2_w = [load_words(tab2_words, 0, "tab2_w0", 0)]
+        w2_raw = keep.tile([P, PASSES, H], I32, name="w2_raw")
+        nc.sync.dma_start(w2_raw[:], w2_words.rearrange("a p c i -> p a (c i)").bitcast(I32))
+        load_packed_planes(nc.sync, w2_s, w2_scales)
+        tab2_w.append(load_words(tab2_words, 1, "tab2_w1", 8192))
+        page = [load_page(0)]
+        idx4 = load_list(offs4, "idx4")
+        page.append(load_page(1))
+        wg1_raw = load_wg(wg1, "wg1_raw")
+        idx1 = load_list(offs, "idx1")
+        tab_w = [load_words(tab_words, a, "tab_w%d" % a, 18432 + 8192 * a) for a in range(PASSES)]
+        page.append(load_page(2))
+        w1_raw = [load_w1(0)]
+        b1_t = keep.tile([P, PACK], F32, name="b1_t")
+        nc.sync.dma_start(b1_t[:], b1.rearrange("(p t) -> p t", t=PACK))
+        w1_raw.append(load_w1(1))
+        idx3 = load_list(offs3, "idx3")
+        page.append(load_page(3))
+        gain_t = keep.tile([P, PACK], F32, name="gain_t")
+        nc.sync.dma_start(gain_t[:], gain.rearrange("(p t) -> p t", t=PACK))
+        idx5 = load_list(offs5, "idx5")
+        stress_t = keep.tile([P, PASSES, PACK], F32, name="stress_t")
+        nc.sync.dma_start(stress_t[:], stress.rearrange("(a p t) -> p a t", a=PASSES, t=PACK))
+        w4_w = keep.tile([P, PASSES, 2 * N], U8, name="w4_w", align_bytes=64)
+        nc.sync.dma_start(w4_w[:].bitcast(I32), w4_words.rearrange("a p c -> p a c").bitcast(I32))
+
+        def deal_wg(raw, name):
+            turned = bank(name + "_turned")
+            for c in range(4):
+                nc.tensor.transpose(turned[:, c, :], raw[:, P * c : P * (c + 1)], ident[:])
+            dealt = []
+            for t in range(PACK):
+                rep = ring.tile([P, 4, 4, 32], F32, name=name + "_rep", tag="wg_rep", bufs=4)
+                src = turned[:].rearrange("p c (i t) -> p t c i", t=PACK)[:, t]
+                nc.scalar.copy(out=rep[:], in_=src.unsqueeze(2).broadcast_to([P, 4, 4, 32]))
+                back = bank(name + "_back")
+                for c in range(4):
+                    nc.tensor.transpose(back[:, c, :], rep[:, c].rearrange("p q i -> p (q i)"), ident[:])
+                w_t = keep.tile([P, S], F32, name="%s_%d" % (name, t))
+                nc.scalar.copy(out=w_t[:], in_=flat(back))
+                dealt.append(w_t)
+            return dealt
+
+        def gather_words(words, idx, name):
+            g = keep.tile([P, S], U32, name=name, align_bytes=64)
+            nc.vector.tensor_copy(g[:], words[:].bitcast(U32).indirect(idx[:]))
+            return g
+
+        def gather_plane(plane, idx, name):
+            g = keep.tile([P, S], U8, name=name, align_bytes=64)
+            nc.vector.tensor_copy(g[:], plane[:].indirect(idx[:]))
+            return g
+
+        def round_weight(raw):
+            wb = ring.tile([P, PACK, P, PACK], BF16, name="wb", tag="wb", bufs=2, align_bytes=64)
+            nc.scalar.copy(out=wb[:].rearrange("p t q j -> p q j t"), in_=raw[:, 0:PACK, :].rearrange("p j (q t) -> p q j t", t=PACK))
+            return wb
+
+        def quantize(src, width, pool, name, bufs):
+            codes = pool.tile([P, width], U32, name=name + "_c", tag=name + "_c", bufs=bufs, align_bytes=64)
+            scales = pool.tile([P, width], U8, name=name + "_s", tag=name + "_s", bufs=bufs, align_bytes=64)
+            nc.vector.quantize_mx(out=codes[:].bitcast(FP8X4), scales=scales[:], in_=src)
+            return codes, scales
+
+        def first_stage(t, weights, moving, func, bias, h):
+            acc = bank("acc")
+            cols = slice(P * t, P * (t + 1))
+            for a in range(PASSES):
+                w_c, w_s = weights[a]
+                v_c, v_s = moving[a]
+                nc.tensor.matmul_mx(
+                    out=flat(acc), lhsT=w_c[:, cols].bitcast(FP8X4), lhsT_scale=w_s[:, cols],
+                    rhs=v_c.bitcast(FP8X4), rhs_scale=v_s, start=(a == 0), stop=(a == PASSES - 1),
+                )
+            nc.scalar.activation(out=h[:], in_=flat(acc), func=func, bias=bias)
+            return h
+
+        def put(t, idx, h, wg_t):
+            nc.vector.tensor_tensor(page[t][:].indirect(idx[:]), h[:], wg_t[:], MULT)
+
+        wg2_t = deal_wg(wg2_raw, "wg2")
+        v2_c = [gather_words(tab2_w[0], idx2, "v2_c0")]
+        v2_s = gather_plane(tab2_s, idx2, "v2_s")
+        w2_c = keep.tile([P, PASSES, PACK, P], U32, name="w2_c", align_bytes=64)
+        nc.vector.tensor_copy(
+            w2_c[:].rearrange("p a t q -> p a q t"), w2_raw[:].bitcast(U32).rearrange("p a (q t) -> p a q t", t=PACK)
+        )
+        w2_sd = keep.tile([P, PACK, P], U8, name="w2_sd", align_bytes=64)
+        nc.vector.tensor_copy(w2_sd[:].rearrange("p t q -> p q t"), w2_s[:].rearrange("p (q t) -> p q t", t=PACK))
+        v2_c.append(gather_words(tab2_w[1], idx2, "v2_c1"))
+        w2_ops = [(w2_c[:, a].rearrange("p t q -> p (t q)"), flat(w2_sd)[4 * a :, :]) for a in range(PASSES)]
+        v2_ops = [(v2_c[a][:], v2_s[4 * a :, :]) for a in range(PASSES)]
+        h2 = [first_stage(t, w2_ops, v2_ops, ACT.Sin, 0.0, keep.tile([P, S], F32, name="h2_%d" % t)) for t in range(PACK)]
+        w3_raw = [load_w3(0), load_w3(1)]
+
+        put(0, idx4, h2[0], wg2_t[0])
+        put(1, idx4, h2[1], wg2_t[1])
+        wg1_t = deal_wg(wg1_raw, "wg1")
+        v1_c = [gather_words(tab_w[0], idx1, "v1_c0")]
+        v1_s = gather_plane(tab_s, idx1, "v1_s")
+        v1_c.append(gather_words(tab_w[1], idx1, "v1_c1"))
+        put(2, idx4, h2[2], wg2_t[2])
+        w1_ops = []
+        for a in range(PASSES):
+            wb = round_weight(w1_raw[a])
+            w_c, w_s = quantize(wb[:].rearrange("p t q j -> p (t q j)"), H, keep, "w1_%d" % a, 1)
+            w1_ops.append((w_c[:], w_s[:]))
+        v1_ops = [(v1_c[a][:], v1_s[4 * a :, :]) for a in range(PASSES)]
+
+        def square_stage(t, h):
+            return first_stage(t, w1_ops, v1_ops, ACT.Square, b1_t[:, t : t + 1], h)
+
+        h1 = square_stage(0, keep.tile([P, S], F32, name="h1_0"))
+        put(3, idx4, h2[3], wg2_t[3])
+        wb3 = [round_weight(w3_raw[a]) for a in range(PASSES)]
+
+        xb = [chain.tile([P, XC, PACK], BF16, name="xb%d" % c, offset=8192 + 2048 * c, align_bytes=64) for c in range(NJ // XC)]
+
+        def scale_plane(t, c, src):
+            nc.scalar.activation(out=xb[c][:, :, t], in_=src, func=ACT.Copy, scale=gain_t[:, t : t + 1])
+
+        w3_ops = []
+        for t in range(PACK - 1):
+            put(t, idx3, h1, wg1_t[t])
+            h1 = square_stage(t + 1, chain.tile([P, S], F32, name="h1_%d" % (t + 1), offset=16384, align_bytes=64))
+            g = ring.tile([P, NJ], F32, name="g", tag="g", bufs=3)
+            nc.vector.tensor_copy(g[:], page[t][:].indirect(idx5[:]))
+            if t == 0:
+                for a in range(PASSES):
+                    w3_ops.append(quantize(wb3[a][:].rearrange("p t q j -> p (t q j)"), 512, keep, "w3_%d" % a, 1))
+            for c in range(NJ // XC):
+                scale_plane(t, c, g[:, XC * c : XC * (c + 1)])
+        last = PACK - 1
+        put(last, idx3, h1, wg1_t[last])
+
+        xq = {}
+        th = {}
+        yq = {}
+
+        def make_x(c):
+            g = ring.tile([P, XC], F32, name="g_last", tag="g_last", bufs=2)
+            nc.vector.tensor_copy(g[:], page[last][:].indirect(idx5[:, (XC // 16) * c : (XC // 16) * (c + 1)]))
+            scale_plane(last, c, g[:])
+
+        def quant_x(c):
+            xq[c] = quantize(xb[c][:].rearrange("p n t -> p (n t)"), XC, keep, "xq%d" % c, 1)
+
+        def third(u):
+            x_c, x_s = xq[u * YC // XC]
+            cols = slice(u * YC % XC, u * YC % XC + YC)
+            for a in range(PASSES):
+                th[u, a] = ring.tile([P, YC, PACK], F32, name="th", tag="th", bufs=6)
+                z = bank("z")
+                w_c, w_s = w3_ops[a]
+                for t in range(PACK):
+                    wc = slice(P * t, P * (t + 1))
+                    nc.tensor.matmul_mx(
+                        out=z[:, t, :], lhsT=w_c[:, wc].bitcast(FP8X4), lhsT_scale=w_s[:, wc],
+                        rhs=x_c[:, cols].bitcast(FP8X4), rhs_scale=x_s[:, cols], start=True, stop=True,
+                    )
+                nc.scalar.activation(out=th[u, a][:], in_=z[:].rearrange("p t n -> p n t"), func=ACT.Tanh)
+
+        yb = {}
+
+        def stress_y(u):
+            yb[u] = ring.tile([P, PASSES, YC, PACK], BF16, name="yb", tag="yb", bufs=3, align_bytes=64)
+            for a in range(PASSES):
+                nc.vector.tensor_tensor(
+                    yb[u][:, a], th[u, a][:], stress_t[:, a].unsqueeze(1).broadcast_to([P, YC, PACK]), MULT
+                )
+
+        def quant_y(u):
+            yq[u] = quantize(yb[u][:].rearrange("p a n t -> p (a n t)"), PASSES * YC, ring, "yq", 3)
+
+        o = {}
+
+        def fourth(u):
+            y_c, y_s = yq[u]
+            parts = 2 if u == n_u - 1 else 1
+            o[u] = [psum.tile([P, 4 // parts, YC], F32, name="o", tag="o", bufs=4) for part in range(parts)]
+            for g_ in range(4):
+                for a in range(PASSES):
+                    nc.tensor.matmul_mx(
+                        out=o[u][g_ * parts // 4][:, g_ % (4 // parts), :],
+                        lhsT=w4_w[:, a, 2 * P * g_ : 2 * P * (g_ + 1)].bitcast(FP4X4),
+                        lhsT_scale=w4_s[:, N * a + P * g_ : N * a + P * (g_ + 1)],
+                        rhs=y_c[:, YC * a : YC * (a + 1)].bitcast(FP8X4),
+                        rhs_scale=y_s[:, YC * a : YC * (a + 1)],
+                        start=(a == 0), stop=(a == PASSES - 1),
+                    )
+
+        out_v = out.rearrange("(g p) j -> p g j", p=P)
+
+        def store(u):
+            parts = len(o[u])
+            rows = 4 // parts
+            for part in range(parts):
+                res = ring.tile([P, rows, YC], F32, name="res", tag="res", bufs=5)
+                if u == n_u - 2 or part == 1:
+                    nc.vector.tensor_copy(res[:], o[u][part][:])
+                else:
+                    nc.scalar.copy(out=res[:], in_=o[u][part][:])
+                nc.sync.dma_start(out_v[:, rows * part : rows * (part + 1), YC * u : YC * (u + 1)], res[:])
+
+        n_u = NJ // YC
+        per = XC // YC
+        make_x(0)
+        make_x(1)
+        quant_x(0)
+        for s in range(n_u + 3):
+            if s % per == 0 and s // per + 2 < NJ // XC:
+                make_x(s // per + 2)
+            if s < n_u:
+                third(s)
+            if 0 <= s - 1 < n_u:
+                stress_y(s - 1)
+            if s % per == 0 and s // per + 1 < NJ // XC:
+                quant_x(s // per + 1)
+            if 0 <= s - 2 < n_u:
+                quant_y(s - 2)
+            if 0 <= s - 3 < n_u:
+                fourth(s - 3)
+            if 0 <= s - 6 < n_u:
+                store(s - 6)
+        for u in range(n_u - 3, n_u):
+            store(u)

@@ -51,17 +51,17 @@ def tile_list_pipe_voicing_ledger_kernel(
         nc.gpsimd.memset(warm[:, 0:1], 0.0)
         nc.scalar.activation(out=warm[:, 1:2], in_=warm[:, 0:1], func=ACT.Silu)
 
-        def zeroed_plane(width, name):
+        def zeroed_plane(width, name, eng):
             t_ = keep.tile([P, width], U8, name=name, align_bytes=64)
-            nc.vector.memset(t_[:].bitcast(I32), 0)
+            eng.memset(t_[:].bitcast(I32), 0)
             return t_
 
-        w2_s = zeroed_plane(H, "w2_s")
-        tab2_s = zeroed_plane(T, "tab2_s")
-        tab_s = zeroed_plane(T, "tab_s")
-        w4_s = zeroed_plane(PASSES * N, "w4_s")
+        tab2_s = zeroed_plane(T, "tab2_s", nc.vector)
+        w2_s = zeroed_plane(H, "w2_s", nc.vector)
         ident = keep.tile([P, P], F32, name="ident")
         make_identity(nc, ident[:])
+        tab_s = zeroed_plane(T, "tab_s", nc.vector)
+        w4_s = zeroed_plane(PASSES * N, "w4_s", nc.vector)
 
         def load_packed_planes(eng, plane, scales):
             for q in range(4):
@@ -92,7 +92,6 @@ def tile_list_pipe_voicing_ledger_kernel(
             nc.sync.dma_start(t_[:, 0:PACK, :], w3[:, 512 * a : 512 * (a + 1)].rearrange("(p j) c -> p j c", j=PACK))
             return t_
 
-        load_packed_planes(nc.gpsimd, tab2_s, tab2_scales)
         load_packed_planes(nc.gpsimd, tab_s, tab_scales)
         for q in range(4):
             nc.gpsimd.dma_start(
@@ -102,6 +101,7 @@ def tile_list_pipe_voicing_ledger_kernel(
 
         idx2 = load_list(offs2, "idx2")
         wg2_raw = load_wg(wg2, "wg2_raw")
+        load_packed_planes(nc.sync, tab2_s, tab2_scales)
         tab2_w = [load_words(tab2_words, 0, "tab2_w0", 0)]
         w2_raw = keep.tile([P, PASSES, H], I32, name="w2_raw")
         nc.sync.dma_start(w2_raw[:], w2_words.rearrange("a p c i -> p a (c i)").bitcast(I32))
@@ -111,13 +111,13 @@ def tile_list_pipe_voicing_ledger_kernel(
         idx4 = load_list(offs4, "idx4")
         page.append(load_page(1))
         wg1_raw = load_wg(wg1, "wg1_raw")
-        idx1 = load_list(offs, "idx1")
-        tab_w = [load_words(tab_words, a, "tab_w%d" % a, 18432 + 8192 * a) for a in range(PASSES)]
         page.append(load_page(2))
-        w1_raw = [load_w1(0)]
+        w1_raw = [load_w1(0), load_w1(1)]
+        idx1 = load_list(offs, "idx1")
+        tab_w = [load_words(tab_words, 0, "tab_w0", 18432)]
         b1_t = keep.tile([P, PACK], F32, name="b1_t")
         nc.sync.dma_start(b1_t[:], b1.rearrange("(p t) -> p t", t=PACK))
-        w1_raw.append(load_w1(1))
+        tab_w.append(load_words(tab_words, 1, "tab_w1", 18432 + 8192))
         idx3 = load_list(offs3, "idx3")
         page.append(load_page(3))
         gain_t = keep.tile([P, PACK], F32, name="gain_t")
@@ -156,7 +156,7 @@ def tile_list_pipe_voicing_ledger_kernel(
             return g
 
         def round_weight(raw):
-            wb = ring.tile([P, PACK, P, PACK], BF16, name="wb", tag="wb", bufs=2, align_bytes=64)
+            wb = ring.tile([P, PACK, P, PACK], BF16, name="wb", tag="wb", bufs=4, align_bytes=64)
             nc.scalar.copy(out=wb[:].rearrange("p t q j -> p q j t"), in_=raw[:, 0:PACK, :].rearrange("p j (q t) -> p q j t", t=PACK))
             return wb
 
@@ -166,21 +166,21 @@ def tile_list_pipe_voicing_ledger_kernel(
             nc.vector.quantize_mx(out=codes[:].bitcast(FP8X4), scales=scales[:], in_=src)
             return codes, scales
 
-        def first_stage(t, weights, moving, func, bias, h):
+        def first_stage(t, weights, moving, func, bias, h, lo=0, hi=S):
             acc = bank("acc")
             cols = slice(P * t, P * (t + 1))
             for a in range(PASSES):
                 w_c, w_s = weights[a]
                 v_c, v_s = moving[a]
                 nc.tensor.matmul_mx(
-                    out=flat(acc), lhsT=w_c[:, cols].bitcast(FP8X4), lhsT_scale=w_s[:, cols],
-                    rhs=v_c.bitcast(FP8X4), rhs_scale=v_s, start=(a == 0), stop=(a == PASSES - 1),
+                    out=flat(acc)[:, 0 : hi - lo], lhsT=w_c[:, cols].bitcast(FP8X4), lhsT_scale=w_s[:, cols],
+                    rhs=v_c[:, lo:hi].bitcast(FP8X4), rhs_scale=v_s[:, lo:hi], start=(a == 0), stop=(a == PASSES - 1),
                 )
-            nc.scalar.activation(out=h[:], in_=flat(acc), func=func, bias=bias)
+            nc.scalar.activation(out=h[:, lo:hi], in_=flat(acc)[:, 0 : hi - lo], func=func, bias=bias)
             return h
 
-        def put(t, idx, h, wg_t):
-            nc.vector.tensor_tensor(page[t][:].indirect(idx[:]), h[:], wg_t[:], MULT)
+        def put(t, idx, h, wg_t, lo=0, hi=S):
+            nc.vector.tensor_tensor(page[t][:].indirect(idx[:, lo // 16 : hi // 16]), h[:, lo:hi], wg_t[:, lo:hi], MULT)
 
         wg2_t = deal_wg(wg2_raw, "wg2")
         v2_c = [gather_words(tab2_w[0], idx2, "v2_c0")]
@@ -191,24 +191,33 @@ def tile_list_pipe_voicing_ledger_kernel(
         )
         w2_sd = keep.tile([P, PACK, P], U8, name="w2_sd", align_bytes=64)
         nc.vector.tensor_copy(w2_sd[:].rearrange("p t q -> p q t"), w2_s[:].rearrange("p (q t) -> p q t", t=PACK))
-        v2_c.append(gather_words(tab2_w[1], idx2, "v2_c1"))
+        half = S // 2
+        v2_c.append(keep.tile([P, S], U32, name="v2_c1", align_bytes=64))
+        for lo in (0, half):
+            nc.vector.tensor_copy(
+                v2_c[1][:, lo : lo + half], tab2_w[1][:].bitcast(U32).indirect(idx2[:, lo // 16 : (lo + half) // 16])
+            )
         w2_ops = [(w2_c[:, a].rearrange("p t q -> p (t q)"), flat(w2_sd)[4 * a :, :]) for a in range(PASSES)]
         v2_ops = [(v2_c[a][:], v2_s[4 * a :, :]) for a in range(PASSES)]
-        h2 = [first_stage(t, w2_ops, v2_ops, ACT.Sin, 0.0, keep.tile([P, S], F32, name="h2_%d" % t)) for t in range(PACK)]
+        h2 = [keep.tile([P, S], F32, name="h2_%d" % t) for t in range(PACK)]
+        for lo in (0, half):
+            first_stage(0, w2_ops, v2_ops, ACT.Sin, 0.0, h2[0], lo, lo + half)
+        for t in range(1, PACK):
+            first_stage(t, w2_ops, v2_ops, ACT.Sin, 0.0, h2[t])
         w3_raw = [load_w3(0), load_w3(1)]
 
-        put(0, idx4, h2[0], wg2_t[0])
+        for lo in (0, half):
+            put(0, idx4, h2[0], wg2_t[0], lo, lo + half)
         put(1, idx4, h2[1], wg2_t[1])
         wg1_t = deal_wg(wg1_raw, "wg1")
-        v1_c = [gather_words(tab_w[0], idx1, "v1_c0")]
-        v1_s = gather_plane(tab_s, idx1, "v1_s")
-        v1_c.append(gather_words(tab_w[1], idx1, "v1_c1"))
         put(2, idx4, h2[2], wg2_t[2])
+        v1_s = gather_plane(tab_s, idx1, "v1_s")
         w1_ops = []
         for a in range(PASSES):
             wb = round_weight(w1_raw[a])
             w_c, w_s = quantize(wb[:].rearrange("p t q j -> p (t q j)"), H, keep, "w1_%d" % a, 1)
             w1_ops.append((w_c[:], w_s[:]))
+        v1_c = [gather_words(tab_w[a], idx1, "v1_c%d" % a) for a in range(PASSES)]
         v1_ops = [(v1_c[a][:], v1_s[4 * a :, :]) for a in range(PASSES)]
 
         def square_stage(t, h):
@@ -218,10 +227,14 @@ def tile_list_pipe_voicing_ledger_kernel(
         put(3, idx4, h2[3], wg2_t[3])
         wb3 = [round_weight(w3_raw[a]) for a in range(PASSES)]
 
-        xb = [chain.tile([P, XC, PACK], BF16, name="xb%d" % c, offset=8192 + 2048 * c, align_bytes=64) for c in range(NJ // XC)]
+        pieces = [(0, YC), (YC, XC)] + [(lo, lo + XC) for lo in range(XC, NJ, XC)]
+        xb = {
+            lo: chain.tile([P, hi - lo, PACK], BF16, name="xb%d" % lo, offset=8192 + 8 * lo, align_bytes=64)
+            for lo, hi in pieces
+        }
 
-        def scale_plane(t, c, src):
-            nc.scalar.activation(out=xb[c][:, :, t], in_=src, func=ACT.Copy, scale=gain_t[:, t : t + 1])
+        def scale_plane(t, lo, src):
+            nc.scalar.activation(out=xb[lo][:, :, t], in_=src, func=ACT.Copy, scale=gain_t[:, t : t + 1])
 
         w3_ops = []
         for t in range(PACK - 1):
@@ -232,8 +245,8 @@ def tile_list_pipe_voicing_ledger_kernel(
             if t == 0:
                 for a in range(PASSES):
                     w3_ops.append(quantize(wb3[a][:].rearrange("p t q j -> p (t q j)"), 512, keep, "w3_%d" % a, 1))
-            for c in range(NJ // XC):
-                scale_plane(t, c, g[:, XC * c : XC * (c + 1)])
+            for lo, hi in pieces:
+                scale_plane(t, lo, g[:, lo:hi])
         last = PACK - 1
         put(last, idx3, h1, wg1_t[last])
 
@@ -244,67 +257,95 @@ def tile_list_pipe_voicing_ledger_kernel(
         def make_x(c):
             g = ring.tile([P, XC], F32, name="g_last", tag="g_last", bufs=2)
             nc.vector.tensor_copy(g[:], page[last][:].indirect(idx5[:, (XC // 16) * c : (XC // 16) * (c + 1)]))
-            scale_plane(last, c, g[:])
+            for lo, hi in pieces:
+                if lo // XC == c:
+                    scale_plane(last, lo, g[:, lo - XC * c : hi - XC * c])
 
         def quant_x(c):
-            xq[c] = quantize(xb[c][:].rearrange("p n t -> p (n t)"), XC, keep, "xq%d" % c, 1)
+            for lo, hi in pieces:
+                if lo // XC == c:
+                    x_c, x_s = quantize(xb[lo][:].rearrange("p n t -> p (n t)"), hi - lo, keep, "xq%d" % lo, 1)
+                    for j in range(lo, hi, YC):
+                        xq[j // YC] = (x_c[:, j - lo : j - lo + YC], x_s[:, j - lo : j - lo + YC])
+
+        n_u = NJ // YC
+        runs = [(0, 1)] + [(u, u + 2) for u in range(1, n_u - 1, 2)] + [(n_u - 1, n_u)]
+        run_of = {u: run for run in runs for u in range(*run)}
 
         def third(u):
-            x_c, x_s = xq[u * YC // XC]
-            cols = slice(u * YC % XC, u * YC % XC + YC)
+            x_c, x_s = xq[u]
+            th[u] = ring.tile([P, PASSES, YC, PACK], F32, name="th", tag="th", bufs=3)
             for a in range(PASSES):
-                th[u, a] = ring.tile([P, YC, PACK], F32, name="th", tag="th", bufs=6)
                 z = bank("z")
                 w_c, w_s = w3_ops[a]
                 for t in range(PACK):
                     wc = slice(P * t, P * (t + 1))
                     nc.tensor.matmul_mx(
                         out=z[:, t, :], lhsT=w_c[:, wc].bitcast(FP8X4), lhsT_scale=w_s[:, wc],
-                        rhs=x_c[:, cols].bitcast(FP8X4), rhs_scale=x_s[:, cols], start=True, stop=True,
+                        rhs=x_c.bitcast(FP8X4), rhs_scale=x_s, start=True, stop=True,
                     )
-                nc.scalar.activation(out=th[u, a][:], in_=z[:].rearrange("p t n -> p n t"), func=ACT.Tanh)
+                nc.scalar.activation(out=th[u][:, a], in_=z[:].rearrange("p t n -> p n t"), func=ACT.Tanh)
 
         yb = {}
 
         def stress_y(u):
             yb[u] = ring.tile([P, PASSES, YC, PACK], BF16, name="yb", tag="yb", bufs=3, align_bytes=64)
-            for a in range(PASSES):
+            step = 1 if u in (0, n_u - 1) else PASSES
+            for a in range(0, PASSES, step):
                 nc.vector.tensor_tensor(
-                    yb[u][:, a], th[u, a][:], stress_t[:, a].unsqueeze(1).broadcast_to([P, YC, PACK]), MULT
+                    yb[u][:, a : a + step], th[u][:, a : a + step],
+                    stress_t[:, a : a + step].unsqueeze(2).broadcast_to([P, step, YC, PACK]), MULT,
                 )
 
         def quant_y(u):
-            yq[u] = quantize(yb[u][:].rearrange("p a n t -> p (a n t)"), PASSES * YC, ring, "yq", 3)
+            if u < n_u - 1:
+                y_c, y_s = quantize(yb[u][:].rearrange("p a n t -> p (a n t)"), PASSES * YC, ring, "yq", 3)
+                yq[u] = [(y_c[:, YC * a : YC * (a + 1)], y_s[:, YC * a : YC * (a + 1)]) for a in range(PASSES)]
+            else:
+                yq[u] = []
+                for a in range(PASSES):
+                    y_c, y_s = quantize(yb[u][:, a].rearrange("p n t -> p (n t)"), YC, keep, "yq_last%d" % a, 1)
+                    yq[u].append((y_c[:], y_s[:]))
 
         o = {}
 
+        def fourth_pass(dst, u, g_, a):
+            y_c, y_s = yq[u][a]
+            nc.tensor.matmul_mx(
+                out=dst,
+                lhsT=w4_w[:, a, 2 * P * g_ : 2 * P * (g_ + 1)].bitcast(FP4X4),
+                lhsT_scale=w4_s[:, N * a + P * g_ : N * a + P * (g_ + 1)],
+                rhs=y_c.bitcast(FP8X4), rhs_scale=y_s, start=(a == 0), stop=(a == PASSES - 1),
+            )
+
         def fourth(u):
-            y_c, y_s = yq[u]
-            parts = 2 if u == n_u - 1 else 1
-            o[u] = [psum.tile([P, 4 // parts, YC], F32, name="o", tag="o", bufs=4) for part in range(parts)]
-            for g_ in range(4):
+            if u < n_u - 1:
+                o[u] = psum.tile([P, 4, YC], F32, name="o", tag="o", bufs=4)
+                for g_ in range(4):
+                    for a in range(PASSES):
+                        fourth_pass(o[u][:, g_, :], u, g_, a)
+            else:
+                o[u] = [psum.tile([P, 4, YC], F32, name="o", tag=tag, bufs=4) for tag in ("bank", "bank", "o", "o")]
                 for a in range(PASSES):
-                    nc.tensor.matmul_mx(
-                        out=o[u][g_ * parts // 4][:, g_ % (4 // parts), :],
-                        lhsT=w4_w[:, a, 2 * P * g_ : 2 * P * (g_ + 1)].bitcast(FP4X4),
-                        lhsT_scale=w4_s[:, N * a + P * g_ : N * a + P * (g_ + 1)],
-                        rhs=y_c[:, YC * a : YC * (a + 1)].bitcast(FP8X4),
-                        rhs_scale=y_s[:, YC * a : YC * (a + 1)],
-                        start=(a == 0), stop=(a == PASSES - 1),
-                    )
+                    for g_ in range(4):
+                        fourth_pass(o[u][g_][:, 0, :], u, g_, a)
 
         out_v = out.rearrange("(g p) j -> p g j", p=P)
 
         def store(u):
-            parts = len(o[u])
-            rows = 4 // parts
-            for part in range(parts):
-                res = ring.tile([P, rows, YC], F32, name="res", tag="res", bufs=5)
-                if u == n_u - 2 or part == 1:
-                    nc.vector.tensor_copy(res[:], o[u][part][:])
-                else:
-                    nc.scalar.copy(out=res[:], in_=o[u][part][:])
-                nc.sync.dma_start(out_v[:, rows * part : rows * (part + 1), YC * u : YC * (u + 1)], res[:])
+            cols = slice(YC * u, YC * (u + 1))
+            if u < n_u - 1:
+                res = ring.tile([P, 4, YC], F32, name="res", tag="res", bufs=4)
+                nc.scalar.copy(out=res[:], in_=o[u][:])
+                nc.sync.dma_start(out_v[:, :, cols], res[:])
+            else:
+                res_v = keep.tile([P, 2, YC], F32, name="res_v")
+                res_s = keep.tile([P, 2, YC], F32, name="res_s")
+                for i in range(2):
+                    nc.vector.tensor_copy(res_v[:, i, :], o[u][i][:, 0, :])
+                    nc.scalar.copy(out=res_s[:, i, :], in_=o[u][2 + i][:, 0, :])
+                nc.sync.dma_start(out_v[:, 0:2, cols], res_v[:])
+                nc.scalar.dma_start(out_v[:, 2:4, cols], res_s[:])
 
         n_u = NJ // YC
         per = XC // YC

@@ -88,16 +88,11 @@ def tile_list_pipe_voicing_ledger_kernel(
             return t_
 
         def load_w3(a):
-            t_ = chain.tile([P, PACK + a, 512], F32, name="w3_raw%d" % a, offset=8192 * a, align_bytes=64)
+            t_ = chain.tile([P, PACK + 1 - a, 512], F32, name="w3_raw%d" % a, offset=10240 * a, align_bytes=64)
             nc.sync.dma_start(t_[:, 0:PACK, :], w3[:, 512 * a : 512 * (a + 1)].rearrange("(p j) c -> p j c", j=PACK))
             return t_
 
         load_packed_planes(nc.gpsimd, tab_s, tab_scales)
-        for q in range(4):
-            nc.gpsimd.dma_start(
-                w4_s[32 * q : 32 * q + 4, :].bitcast(I32).rearrange("r (a n) -> r a n", a=PASSES),
-                w4_scales[:, 4 * q : 4 * q + 4, :].bitcast(I32).rearrange("a r n -> r a n"),
-            )
 
         idx2 = load_list(offs2, "idx2")
         wg2_raw = load_wg(wg2, "wg2_raw")
@@ -106,20 +101,20 @@ def tile_list_pipe_voicing_ledger_kernel(
         w2_raw = keep.tile([P, PASSES, H], I32, name="w2_raw")
         nc.sync.dma_start(w2_raw[:], w2_words.rearrange("a p c i -> p a (c i)").bitcast(I32))
         load_packed_planes(nc.sync, w2_s, w2_scales)
-        tab2_w.append(load_words(tab2_words, 1, "tab2_w1", 8192))
+        tab2_w.append(load_words(tab2_words, 1, "tab2_w1", 10240))
         page = [load_page(0)]
         idx4 = load_list(offs4, "idx4")
         page.append(load_page(1))
-        wg1_raw = load_wg(wg1, "wg1_raw")
         page.append(load_page(2))
         w1_raw = [load_w1(0), load_w1(1)]
+        wg1_raw = load_wg(wg1, "wg1_raw")
         idx1 = load_list(offs, "idx1")
         tab_w = [load_words(tab_words, 0, "tab_w0", 18432)]
         b1_t = keep.tile([P, PACK], F32, name="b1_t")
         nc.sync.dma_start(b1_t[:], b1.rearrange("(p t) -> p t", t=PACK))
         tab_w.append(load_words(tab_words, 1, "tab_w1", 18432 + 8192))
-        idx3 = load_list(offs3, "idx3")
         page.append(load_page(3))
+        idx3 = load_list(offs3, "idx3")
         gain_t = keep.tile([P, PACK], F32, name="gain_t")
         nc.sync.dma_start(gain_t[:], gain.rearrange("(p t) -> p t", t=PACK))
         idx5 = load_list(offs5, "idx5")
@@ -157,7 +152,7 @@ def tile_list_pipe_voicing_ledger_kernel(
 
         def round_weight(raw):
             wb = ring.tile([P, PACK, P, PACK], BF16, name="wb", tag="wb", bufs=4, align_bytes=64)
-            nc.scalar.copy(out=wb[:].rearrange("p t q j -> p q j t"), in_=raw[:, 0:PACK, :].rearrange("p j (q t) -> p q j t", t=PACK))
+            nc.scalar.copy(out=wb[:].rearrange("p t q j -> p q t j"), in_=raw[:, 0:PACK, :].rearrange("p j (q t) -> p q t j", t=PACK))
             return wb
 
         def quantize(src, width, pool, name, bufs):
@@ -187,10 +182,10 @@ def tile_list_pipe_voicing_ledger_kernel(
         v2_s = gather_plane(tab2_s, idx2, "v2_s")
         w2_c = keep.tile([P, PASSES, PACK, P], U32, name="w2_c", align_bytes=64)
         nc.vector.tensor_copy(
-            w2_c[:].rearrange("p a t q -> p a q t"), w2_raw[:].bitcast(U32).rearrange("p a (q t) -> p a q t", t=PACK)
+            w2_c[:], w2_raw[:].bitcast(U32).rearrange("p a (q t) -> p a t q", t=PACK)
         )
         w2_sd = keep.tile([P, PACK, P], U8, name="w2_sd", align_bytes=64)
-        nc.vector.tensor_copy(w2_sd[:].rearrange("p t q -> p q t"), w2_s[:].rearrange("p (q t) -> p q t", t=PACK))
+        nc.vector.tensor_copy(w2_sd[:], w2_s[:].rearrange("p (q t) -> p t q", t=PACK))
         half = S // 2
         v2_c.append(keep.tile([P, S], U32, name="v2_c1", align_bytes=64))
         for lo in (0, half):
@@ -205,11 +200,15 @@ def tile_list_pipe_voicing_ledger_kernel(
         for t in range(1, PACK):
             first_stage(t, w2_ops, v2_ops, ACT.Sin, 0.0, h2[t])
         w3_raw = [load_w3(0), load_w3(1)]
+        for q in range(4):
+            nc.sync.dma_start(
+                w4_s[32 * q : 32 * q + 4, :].bitcast(I32).rearrange("r (a n) -> r a n", a=PASSES),
+                w4_scales[:, 4 * q : 4 * q + 4, :].bitcast(I32).rearrange("a r n -> r a n"),
+            )
 
         for lo in (0, half):
             put(0, idx4, h2[0], wg2_t[0], lo, lo + half)
         put(1, idx4, h2[1], wg2_t[1])
-        wg1_t = deal_wg(wg1_raw, "wg1")
         put(2, idx4, h2[2], wg2_t[2])
         v1_s = gather_plane(tab_s, idx1, "v1_s")
         w1_ops = []
@@ -217,6 +216,7 @@ def tile_list_pipe_voicing_ledger_kernel(
             wb = round_weight(w1_raw[a])
             w_c, w_s = quantize(wb[:].rearrange("p t q j -> p (t q j)"), H, keep, "w1_%d" % a, 1)
             w1_ops.append((w_c[:], w_s[:]))
+        wg1_t = deal_wg(wg1_raw, "wg1")
         v1_c = [gather_words(tab_w[a], idx1, "v1_c%d" % a) for a in range(PASSES)]
         v1_ops = [(v1_c[a][:], v1_s[4 * a :, :]) for a in range(PASSES)]
 
@@ -229,7 +229,7 @@ def tile_list_pipe_voicing_ledger_kernel(
 
         pieces = [(0, YC), (YC, XC)] + [(lo, lo + XC) for lo in range(XC, NJ, XC)]
         xb = {
-            lo: chain.tile([P, hi - lo, PACK], BF16, name="xb%d" % lo, offset=8192 + 8 * lo, align_bytes=64)
+            lo: chain.tile([P, hi - lo, PACK], BF16, name="xb%d" % lo, offset=10240 + 8 * lo, align_bytes=64)
             for lo, hi in pieces
         }
 
@@ -239,7 +239,7 @@ def tile_list_pipe_voicing_ledger_kernel(
         w3_ops = []
         for t in range(PACK - 1):
             put(t, idx3, h1, wg1_t[t])
-            h1 = square_stage(t + 1, chain.tile([P, S], F32, name="h1_%d" % (t + 1), offset=16384, align_bytes=64))
+            h1 = square_stage(t + 1, chain.tile([P, S], F32, name="h1_%d" % (t + 1), offset=8192, align_bytes=64))
             g = ring.tile([P, NJ], F32, name="g", tag="g", bufs=3)
             nc.vector.tensor_copy(g[:], page[t][:].indirect(idx5[:]))
             if t == 0:

@@ -92,11 +92,13 @@ def tile_list_pipe_voicing_ledger_kernel(
             nc.sync.dma_start(t_[:, 0:PACK, :], w3[:, 512 * a : 512 * (a + 1)].rearrange("(p j) c -> p j c", j=PACK))
             return t_
 
+        load_packed_planes(nc.gpsimd, tab2_s, tab2_scales)
         load_packed_planes(nc.gpsimd, tab_s, tab_scales)
+        b1_t = keep.tile([P, PACK], F32, name="b1_t")
+        nc.gpsimd.dma_start(b1_t[:], b1.rearrange("(p t) -> p t", t=PACK))
 
         idx2 = load_list(offs2, "idx2")
         wg2_raw = load_wg(wg2, "wg2_raw")
-        load_packed_planes(nc.sync, tab2_s, tab2_scales)
         tab2_w = [load_words(tab2_words, 0, "tab2_w0", 0)]
         w2_raw = keep.tile([P, PASSES, H], I32, name="w2_raw")
         nc.sync.dma_start(w2_raw[:], w2_words.rearrange("a p c i -> p a (c i)").bitcast(I32))
@@ -110,8 +112,6 @@ def tile_list_pipe_voicing_ledger_kernel(
         wg1_raw = load_wg(wg1, "wg1_raw")
         idx1 = load_list(offs, "idx1")
         tab_w = [load_words(tab_words, 0, "tab_w0", 18432)]
-        b1_t = keep.tile([P, PACK], F32, name="b1_t")
-        nc.sync.dma_start(b1_t[:], b1.rearrange("(p t) -> p t", t=PACK))
         tab_w.append(load_words(tab_words, 1, "tab_w1", 18432 + 8192))
         page.append(load_page(3))
         idx3 = load_list(offs3, "idx3")

from contextlib import ExitStack

import concourse.mybir as mybir
from concourse.masks import make_identity

F32 = mybir.dt.float32
BF16 = mybir.dt.bfloat16
I32 = mybir.dt.int32
U32 = mybir.dt.uint32
U16 = mybir.dt.uint16
U8 = mybir.dt.uint8
FP8X4 = mybir.dt.float8_e4m3fn_x4
FP4X4 = mybir.dt.float4_e2m1fn_x4
ACT = mybir.ActivationFunctionType
MULT = mybir.AluOpType.mult

K, T, S, T2, NJ, H, M, N = 1024, 2048, 512, 2048, 1024, 512, 1024, 512
FLOPS = 2 * (2 * K * H * S + H * M * NJ + M * N * NJ)

P = 128
PACK = 4
PASSES = 2
XC = 256
YC = 128


def tile_list_pipe_voicing_ledger_kernel(
    tc, tab_words, tab_scales, tab2_words, tab2_scales, offs, offs2, offs3, offs4, offs5,
    w1, b1, w2_words, w2_scales, wg1, wg2, page0, gain, w3, stress, w4_words, w4_scales, out,
):
    nc = tc.nc
    with ExitStack() as ctx:
        lists = ctx.enter_context(tc.tile_pool(name="lists", bufs=1))
        keep = ctx.enter_context(tc.tile_pool(name="keep", bufs=1))
        ring = ctx.enter_context(tc.tile_pool(name="ring", bufs=2))
        chain = ctx.enter_context(tc.tile_pool(name="chain", bufs=1))
        psum = ctx.enter_context(tc.psum_pool(name="psum", bufs=1))

        def load_list(src, name):
            t_ = lists.tile(list(src.shape), U16, name=name)
            nc.sync.dma_start(t_[:], src)
            return t_

        def bank(name):
            return psum.tile([P, PACK, P], F32, name=name, tag="bank", bufs=4)

        def flat(t_):
            return t_[:].rearrange("p a b -> p (a b)")

        warm = keep.tile([P, 8], F32, name="warm")
        nc.gpsimd.memset(warm[:, 0:1], 0.0)
        nc.scalar.activation(out=warm[:, 1:2], in_=warm[:, 0:1], func=ACT.Silu)

        def zeroed_plane(width, name, eng):
            t_ = keep.tile([P, width], U8, name=name, align_bytes=64)
            eng.memset(t_[:].bitcast(I32), 0)
            return t_

        tab2_s = zeroed_plane(T, "tab2_s", nc.vector)
        w2_s = zeroed_plane(H, "w2_s", nc.vector)
        ident = keep.tile([P, P], F32, name="ident")
        make_identity(nc, ident[:])
        tab_s = zeroed_plane(T, "tab_s", nc.vector)
        w4_s = zeroed_plane(PASSES * N, "w4_s", nc.vector)

        def load_packed_planes(eng, plane, scales):
            for q in range(4):
                eng.dma_start(plane[32 * q : 32 * q + 8, :].bitcast(I32), scales[:, 4 * q : 4 * q + 4, :].bitcast(I32))

        def load_words(src, a, name, offset):
            t_ = chain.tile([P, T], I32, name=name, offset=offset, align_bytes=64)
            nc.sync.dma_start(t_[:], src[a].rearrange("p c i -> p (c i)").bitcast(I32))
            return t_

        def load_page(t):
            t_ = keep.tile([P, T2], F32, name="page%d" % t)
            nc.sync.dma_start(t_[:], page0.rearrange("(p t) s -> t p s", t=PACK)[t])
            return t_

        def load_wg(src, name):
            t_ = keep.tile([P, S], F32, name=name)
            nc.sync.dma_start(t_[:], src)
            return t_

        def load_w1(a):
            t_ = keep.tile([P, PACK, H], F32, name="w1_raw%d" % a)
            nc.sync.dma_start(t_[:], w1[512 * a : 512 * (a + 1), :].rearrange("(p j) c -> p j c", j=PACK))
            return t_

        def load_w3(a):
            t_ = chain.tile([P, PACK + 1 - a, 512], F32, name="w3_raw%d" % a, offset=10240 * a, align_bytes=64)
            nc.sync.dma_start(t_[:, 0:PACK, :], w3[:, 512 * a : 512 * (a + 1)].rearrange("(p j) c -> p j c", j=PACK))
            return t_

        load_packed_planes(nc.gpsimd, tab2_s, tab2_scales)
        load_packed_planes(nc.gpsimd, tab_s, tab_scales)
        b1_t = keep.tile([P, PACK], F32, name="b1_t")
        nc.gpsimd.dma_start(b1_t[:], b1.rearrange("(p t) -> p t", t=PACK))

        idx2 = load_list(offs2, "idx2")
        wg2_raw = load_wg(wg2, "wg2_raw")
        tab2_w = [load_words(tab2_words, 0, "tab2_w0", 0)]
        w2_raw = keep.tile([P, PASSES, H], I32, name="w2_raw")
        nc.sync.dma_start(w2_raw[:], w2_words.rearrange("a p c i -> p a (c i)").bitcast(I32))
        load_packed_planes(nc.sync, w2_s, w2_scales)
        tab2_w.append(load_words(tab2_words, 1, "tab2_w1", 10240))
        page = [load_page(0)]
        idx4 = load_list(offs4, "idx4")
        page.append(load_page(1))
        page.append(load_page(2))
        w1_raw = [load_w1(0), load_w1(1)]
        wg1_raw = load_wg(wg1, "wg1_raw")
        idx1 = load_list(offs, "idx1")
        tab_w = [load_words(tab_words, 0, "tab_w0", 18432)]
        tab_w.append(load_words(tab_words, 1, "tab_w1", 18432 + 8192))
        page.append(load_page(3))
        idx3 = load_list(offs3, "idx3")
        gain_t = keep.tile([P, PACK], F32, name="gain_t")
        nc.sync.dma_start(gain_t[:], gain.rearrange("(p t) -> p t", t=PACK))
        idx5 = load_list(offs5, "idx5")
        stress_t = keep.tile([P, PASSES, PACK], F32, name="stress_t")
        nc.sync.dma_start(stress_t[:], stress.rearrange("(a p t) -> p a t", a=PASSES, t=PACK))
        w4_w = keep.tile([P, PASSES, 2 * N], U8, name="w4_w", align_bytes=64)
        nc.sync.dma_start(w4_w[:].bitcast(I32), w4_words.rearrange("a p c -> p a c").bitcast(I32))

        def deal_wg(raw, name):
            turned = bank(name + "_turned")
            for c in range(4):
                nc.tensor.transpose(turned[:, c, :], raw[:, P * c : P * (c + 1)], ident[:])
            dealt = []
            for t in range(PACK):
                rep = ring.tile([P, 4, 4, 32], F32, name=name + "_rep", tag="wg_rep", bufs=4)
                src = turned[:].rearrange("p c (i t) -> p t c i", t=PACK)[:, t]
                nc.scalar.copy(out=rep[:], in_=src.unsqueeze(2).broadcast_to([P, 4, 4, 32]))
                back = bank(name + "_back")
                for c in range(4):
                    nc.tensor.transpose(back[:, c, :], rep[:, c].rearrange("p q i -> p (q i)"), ident[:])
                w_t = keep.tile([P, S], F32, name="%s_%d" % (name, t))
                nc.scalar.copy(out=w_t[:], in_=flat(back))
                dealt.append(w_t)
            return dealt

        def gather_words(words, idx, name):
            g = keep.tile([P, S], U32, name=name, align_bytes=64)
            nc.vector.tensor_copy(g[:], words[:].bitcast(U32).indirect(idx[:]))
            return g

        def gather_plane(plane, idx, name):
            g = keep.tile([P, S], U8, name=name, align_bytes=64)
            nc.vector.tensor_copy(g[:], plane[:].indirect(idx[:]))
            return g

        def round_weight(raw):
            wb = ring.tile([P, PACK, P, PACK], BF16, name="wb", tag="wb", bufs=4, align_bytes=64)
            nc.scalar.copy(out=wb[:].rearrange("p t q j -> p q t j"), in_=raw[:, 0:PACK, :].rearrange("p j (q t) -> p q t j", t=PACK))
            return wb

        def quantize(src, width, pool, name, bufs):
            codes = pool.tile([P, width], U32, name=name + "_c", tag=name + "_c", bufs=bufs, align_bytes=64)
            scales = pool.tile([P, width], U8, name=name + "_s", tag=name + "_s", bufs=bufs, align_bytes=64)
            nc.vector.quantize_mx(out=codes[:].bitcast(FP8X4), scales=scales[:], in_=src)
            return codes, scales

        def first_stage(t, weights, moving, func, bias, h, lo=0, hi=S):
            acc = bank("acc")
            cols = slice(P * t, P * (t + 1))
            for a in range(PASSES):
                w_c, w_s = weights[a]
                v_c, v_s = moving[a]
                nc.tensor.matmul_mx(
                    out=flat(acc)[:, 0 : hi - lo], lhsT=w_c[:, cols].bitcast(FP8X4), lhsT_scale=w_s[:, cols],
                    rhs=v_c[:, lo:hi].bitcast(FP8X4), rhs_scale=v_s[:, lo:hi], start=(a == 0), stop=(a == PASSES - 1),
                )
            nc.scalar.activation(out=h[:, lo:hi], in_=flat(acc)[:, 0 : hi - lo], func=func, bias=bias)
            return h

        def put(t, idx, h, wg_t, lo=0, hi=S):
            nc.vector.tensor_tensor(page[t][:].indirect(idx[:, lo // 16 : hi // 16]), h[:, lo:hi], wg_t[:, lo:hi], MULT)

        wg2_t = deal_wg(wg2_raw, "wg2")
        v2_c = [gather_words(tab2_w[0], idx2, "v2_c0")]
        v2_s = gather_plane(tab2_s, idx2, "v2_s")
        w2_c = keep.tile([P, PASSES, PACK, P], U32, name="w2_c", align_bytes=64)
        nc.vector.tensor_copy(
            w2_c[:], w2_raw[:].bitcast(U32).rearrange("p a (q t) -> p a t q", t=PACK)
        )
        w2_sd = keep.tile([P, PACK, P], U8, name="w2_sd", align_bytes=64)
        nc.vector.tensor_copy(w2_sd[:], w2_s[:].rearrange("p (q t) -> p t q", t=PACK))
        half = S // 2
        v2_c.append(keep.tile([P, S], U32, name="v2_c1", align_bytes=64))
        for lo in (0, half):
            nc.vector.tensor_copy(
                v2_c[1][:, lo : lo + half], tab2_w[1][:].bitcast(U32).indirect(idx2[:, lo // 16 : (lo + half) // 16])
            )
        w2_ops = [(w2_c[:, a].rearrange("p t q -> p (t q)"), flat(w2_sd)[4 * a :, :]) for a in range(PASSES)]
        v2_ops = [(v2_c[a][:], v2_s[4 * a :, :]) for a in range(PASSES)]
        h2 = [keep.tile([P, S], F32, name="h2_%d" % t) for t in range(PACK)]
        for lo in (0, half):
            first_stage(0, w2_ops, v2_ops, ACT.Sin, 0.0, h2[0], lo, lo + half)
        for t in range(1, PACK):
            first_stage(t, w2_ops, v2_ops, ACT.Sin, 0.0, h2[t])
        w3_raw = [load_w3(0), load_w3(1)]
        for q in range(4):
            nc.sync.dma_start(
                w4_s[32 * q : 32 * q + 4, :].bitcast(I32).rearrange("r (a n) -> r a n", a=PASSES),
                w4_scales[:, 4 * q : 4 * q + 4, :].bitcast(I32).rearrange("a r n -> r a n"),
            )

        for lo in (0, half):
            put(0, idx4, h2[0], wg2_t[0], lo, lo + half)
        put(1, idx4, h2[1], wg2_t[1])
        put(2, idx4, h2[2], wg2_t[2])
        v1_s = gather_plane(tab_s, idx1, "v1_s")
        w1_ops = []
        for a in range(PASSES):
            wb = round_weight(w1_raw[a])
            w_c, w_s = quantize(wb[:].rearrange("p t q j -> p (t q j)"), H, keep, "w1_%d" % a, 1)
            w1_ops.append((w_c[:], w_s[:]))
        wg1_t = deal_wg(wg1_raw, "wg1")
        v1_c = [gather_words(tab_w[a], idx1, "v1_c%d" % a) for a in range(PASSES)]
        v1_ops = [(v1_c[a][:], v1_s[4 * a :, :]) for a in range(PASSES)]

        def square_stage(t, h):
            return first_stage(t, w1_ops, v1_ops, ACT.Square, b1_t[:, t : t + 1], h)

        h1 = square_stage(0, keep.tile([P, S], F32, name="h1_0"))
        put(3, idx4, h2[3], wg2_t[3])
        wb3 = [round_weight(w3_raw[a]) for a in range(PASSES)]

        pieces = [(0, YC), (YC, XC)] + [(lo, lo + XC) for lo in range(XC, NJ, XC)]
        xb = {
            lo: chain.tile([P, hi - lo, PACK], BF16, name="xb%d" % lo, offset=10240 + 8 * lo, align_bytes=64)
            for lo, hi in pieces
        }

        def scale_plane(t, lo, src):
            nc.scalar.activation(out=xb[lo][:, :, t], in_=src, func=ACT.Copy, scale=gain_t[:, t : t + 1])

        w3_ops = []
        for t in range(PACK - 1):
            put(t, idx3, h1, wg1_t[t])
            h1 = square_stage(t + 1, chain.tile([P, S], F32, name="h1_%d" % (t + 1), offset=8192, align_bytes=64))
            g = ring.tile([P, NJ], F32, name="g", tag="g", bufs=3)
            nc.vector.tensor_copy(g[:], page[t][:].indirect(idx5[:]))
            if t == 0:
                for a in range(PASSES):
                    w3_ops.append(quantize(wb3[a][:].rearrange("p t q j -> p (t q j)"), 512, keep, "w3_%d" % a, 1))
            for lo, hi in pieces:
                scale_plane(t, lo, g[:, lo:hi])
        last = PACK - 1
        put(last, idx3, h1, wg1_t[last])

        xq = {}
        th = {}
        yq = {}

        def make_x(c):
            g = ring.tile([P, XC], F32, name="g_last", tag="g_last", bufs=2)
            nc.vector.tensor_copy(g[:], page[last][:].indirect(idx5[:, (XC // 16) * c : (XC // 16) * (c + 1)]))
            for lo, hi in pieces:
                if lo // XC == c:
                    scale_plane(last, lo, g[:, lo - XC * c : hi - XC * c])

        def quant_x(c):
            for lo, hi in pieces:
                if lo // XC == c:
                    x_c, x_s = quantize(xb[lo][:].rearrange("p n t -> p (n t)"), hi - lo, keep, "xq%d" % lo, 1)
                    for j in range(lo, hi, YC):
                        xq[j // YC] = (x_c[:, j - lo : j - lo + YC], x_s[:, j - lo : j - lo + YC])

        n_u = NJ // YC
        runs = [(0, 1)] + [(u, u + 2) for u in range(1, n_u - 1, 2)] + [(n_u - 1, n_u)]
        run_of = {u: run for run in runs for u in range(*run)}

        def third(u):
            x_c, x_s = xq[u]
            th[u] = ring.tile([P, PASSES, YC, PACK], F32, name="th", tag="th", bufs=3)
            for a in range(PASSES):
                z = bank("z")
                w_c, w_s = w3_ops[a]
                for t in range(PACK):
                    wc = slice(P * t, P * (t + 1))
                    nc.tensor.matmul_mx(
                        out=z[:, t, :], lhsT=w_c[:, wc].bitcast(FP8X4), lhsT_scale=w_s[:, wc],
                        rhs=x_c.bitcast(FP8X4), rhs_scale=x_s, start=True, stop=True,
                    )
                nc.scalar.activation(out=th[u][:, a], in_=z[:].rearrange("p t n -> p n t"), func=ACT.Tanh)

        yb = {}

        def stress_y(u):
            yb[u] = ring.tile([P, PASSES, YC, PACK], BF16, name="yb", tag="yb", bufs=3, align_bytes=64)
            step = 1 if u in (0, n_u - 1) else PASSES
            for a in range(0, PASSES, step):
                nc.vector.tensor_tensor(
                    yb[u][:, a : a + step], th[u][:, a : a + step],
                    stress_t[:, a : a + step].unsqueeze(2).broadcast_to([P, step, YC, PACK]), MULT,
                )

        def quant_y(u):
            if u < n_u - 1:
                y_c, y_s = quantize(yb[u][:].rearrange("p a n t -> p (a n t)"), PASSES * YC, ring, "yq", 3)
                yq[u] = [(y_c[:, YC * a : YC * (a + 1)], y_s[:, YC * a : YC * (a + 1)]) for a in range(PASSES)]
            else:
                yq[u] = []
                for a in range(PASSES):
                    y_c, y_s = quantize(yb[u][:, a].rearrange("p n t -> p (n t)"), YC, keep, "yq_last%d" % a, 1)
                    yq[u].append((y_c[:], y_s[:]))

        o = {}

        def fourth_pass(dst, u, g_, a):
            y_c, y_s = yq[u][a]
            nc.tensor.matmul_mx(
                out=dst,
                lhsT=w4_w[:, a, 2 * P * g_ : 2 * P * (g_ + 1)].bitcast(FP4X4),
                lhsT_scale=w4_s[:, N * a + P * g_ : N * a + P * (g_ + 1)],
                rhs=y_c.bitcast(FP8X4), rhs_scale=y_s, start=(a == 0), stop=(a == PASSES - 1),
            )

        def fourth(u):
            if u < n_u - 1:
                o[u] = psum.tile([P, 4, YC], F32, name="o", tag="o", bufs=4)
                for g_ in range(4):
                    for a in range(PASSES):
                        fourth_pass(o[u][:, g_, :], u, g_, a)
            else:
                o[u] = [psum.tile([P, 4, YC], F32, name="o", tag=tag, bufs=4) for tag in ("bank", "bank", "o", "o")]
                for a in range(PASSES):
                    for g_ in range(4):
                        fourth_pass(o[u][g_][:, 0, :], u, g_, a)

        out_v = out.rearrange("(g p) j -> p g j", p=P)

        def store(u):
            cols = slice(YC * u, YC * (u + 1))
            if u < n_u - 1:
                res = ring.tile([P, 4, YC], F32, name="res", tag="res", bufs=4)
                nc.scalar.copy(out=res[:], in_=o[u][:])
                nc.sync.dma_start(out_v[:, :, cols], res[:])
            else:
                res_v = keep.tile([P, 2, YC], F32, name="res_v")
                res_s = keep.tile([P, 2, YC], F32, name="res_s")
                for i in range(2):
                    nc.vector.tensor_copy(res_v[:, i, :], o[u][i][:, 0, :])
                    nc.scalar.copy(out=res_s[:, i, :], in_=o[u][2 + i][:, 0, :])
                nc.sync.dma_start(out_v[:, 0:2, cols], res_v[:])
                nc.scalar.dma_start(out_v[:, 2:4, cols], res_s[:])

        n_u = NJ // YC
        per = XC // YC
        make_x(0)
        make_x(1)
        quant_x(0)
        for s in range(n_u + 3):
            if s % per == 0 and s // per + 2 < NJ // XC:
                make_x(s // per + 2)
            if s < n_u:
                third(s)
            if 0 <= s - 1 < n_u:
                stress_y(s - 1)
            if s % per == 0 and s // per + 1 < NJ // XC:
                quant_x(s // per + 1)
            if 0 <= s - 2 < n_u:
                quant_y(s - 2)
            if 0 <= s - 3 < n_u:
                fourth(s - 3)
            if 0 <= s - 6 < n_u:
                store(s - 6)
        for u in range(n_u - 3, n_u):
            store(u)
